import numpy as np
import ml_dtypes


def mxq(x, axis, fmt="e4m3"):
    dtype, down = {"e4m3": (ml_dtypes.float8_e4m3fn, 7), "e5m2": (ml_dtypes.float8_e5m2, 14)}[fmt]
    v = np.moveaxis(np.asarray(x, np.float32).astype(ml_dtypes.bfloat16).astype(np.float64), axis, -1)
    blocks = v.reshape(v.shape[:-1] + (-1, 32))
    amax = np.abs(blocks).max(-1, keepdims=True)
    byte = np.maximum(np.where(amax > 0, np.frexp(amax)[1] - 1 + 127, 0) - down, 1)
    scale = np.exp2(byte - 127.0)
    codes = (blocks / scale).astype(np.float32).astype(dtype).astype(np.float64)
    return np.moveaxis((codes * scale).reshape(v.shape), -1, axis)


WIDE = False


def mx_kscale(k):
    if not WIDE:
        return np.ones(k)
    levels = np.array([10, -10, 5, -5, 0])
    if k % 512:
        return np.exp2(np.random.permutation(np.resize(levels, k // 32))).repeat(32)
    a = np.empty((k // 512, 16))
    for p in range(k // 512):
        a[p, :8] = np.random.permutation(np.resize(levels, 8))
        for g in range(8):
            far = levels[np.abs(levels - a[p, g]) >= 10]
            a[p, g + 8] = far[np.random.randint(len(far))]
    return np.exp2(a.ravel()).repeat(32)


def f64(x):
    return np.asarray(x).astype(np.float64)


def striped(idx):
    return np.tile(idx.reshape(-1, 16).T, (8, 1)).astype(np.uint16)


def unstriped(offs):
    return offs[:16].T.reshape(-1).astype(np.int64)


def pack_weight(w):
    k, n = w.shape
    w = f64(np.asarray(w, np.float32).astype(ml_dtypes.bfloat16)).reshape(k // 32, 32, n)
    amax = np.abs(w).max(1)
    byte = np.clip(np.where(amax > 0, np.frexp(amax)[1] - 1 + 127 - 7, 1), 1, 254)
    scaled = (w * np.exp2(127.0 - byte)[:, None, :]).reshape(k, n).astype(np.float32)
    words = np.ascontiguousarray(scaled.reshape(k // 512, 128, 4, n).transpose(0, 1, 3, 2)).astype(ml_dtypes.float8_e4m3fn).view(np.uint8)
    return words, np.ascontiguousarray(byte.astype(np.uint8).reshape(k // 512, 16, n))


def unpack_weight(words, scales):
    g, p, n, _ = words.shape
    vals = np.ascontiguousarray(words).view(ml_dtypes.float8_e4m3fn).astype(np.float64) * np.repeat(np.exp2(scales.astype(np.float64) - 127.0), 8, axis=1)[..., None]
    return vals.transpose(0, 1, 3, 2).reshape(g * 512, n)


E2M1 = np.array([0.0, 0.5, 1.0, 1.5, 2.0, 3.0, 4.0, 6.0, -0.0, -0.5, -1.0, -1.5, -2.0, -3.0, -4.0, -6.0])


def pack_fp4(w):
    k, n = w.shape
    w = f64(np.asarray(w, np.float32).astype(ml_dtypes.bfloat16)).reshape(k // 32, 32, n)
    amax = np.abs(w).max(1)
    mant, ex = np.frexp(amax / 6.0)
    byte = np.clip(np.where(amax > 0, np.where(mant > 0.5, ex, ex - 1) + 127, 1), 1, 254)
    scaled = (w * np.exp2(127.0 - byte)[:, None, :]).reshape(k, n).astype(np.float32)
    c = np.ascontiguousarray(scaled.reshape(k // 512, 128, 4, n).transpose(0, 1, 3, 2)).astype(ml_dtypes.float4_e2m1fn).view(np.uint8) & 0xF
    words = (c[..., 0::2] | (c[..., 1::2] << 4)).reshape(k // 512, 128, 2 * n)
    return np.ascontiguousarray(words), np.ascontiguousarray(byte.astype(np.uint8).reshape(k // 512, 16, n))


def unpack_fp4(words, scales):
    g, _, n = scales.shape
    words = np.ascontiguousarray(words).reshape(g, 128, n, 2)
    nib = np.empty((g, 128, n, 4), np.uint8)
    nib[..., 0::2] = words & 0xF
    nib[..., 1::2] = words >> 4
    vals = E2M1[nib] * np.repeat(np.exp2(scales.astype(np.float64) - 127.0), 8, axis=1)[..., None]
    return vals.transpose(0, 1, 3, 2).reshape(g * 512, n)


def planes(y):
    n, m = y.shape
    v = y.astype(np.float32).astype(ml_dtypes.bfloat16).astype(np.float64).reshape(n // 32, 32, m)
    top = np.abs(v).max(1)
    byte = np.clip(np.where(top > 0, np.frexp(top)[1] - 1 + 127 - 7, 1), 1, 254)
    codes = (v * np.exp2(127.0 - byte)[:, None, :]).reshape(n, m).astype(np.float32).astype(ml_dtypes.float8_e4m3fn).view(np.uint8)
    words = codes.reshape(n // 512, 128, 4, m).transpose(0, 1, 3, 2)
    return np.ascontiguousarray(words), np.ascontiguousarray(byte.astype(np.uint8).reshape(n // 512, 16, m))


K, T, S, N, H, U = 1024, 1024, 512, 512, 512, 1024


def setup_inputs():
    n = np.random.standard_normal
    s = mx_kscale(K)[:, None]
    u = mx_kscale(H)
    packed_xT = pack_weight(n((K, T)) * s)
    packed_w1 = pack_fp4(n((K, N)) / np.sqrt(K) / s)
    packed_w2 = pack_fp4(n((H, N)) / np.sqrt(H) / u[:, None])
    return {
        "x_words": packed_xT[0],
        "x_scales": packed_xT[1],
        "w1_words": packed_w1[0],
        "w1_scales": packed_w1[1],
        "wm": (np.random.uniform(0.1, 0.9, (H, U))).astype(np.float32),
        "unit": (np.random.uniform(0.6, 1.4, (H, 1)) * u[:, None]).astype(np.float32),
        "w2_words": packed_w2[0],
        "w2_scales": packed_w2[1],
        "offs": striped(np.random.permutation(T)[:S]),
        "c1": striped(np.random.permutation(np.concatenate([np.arange(S), np.random.randint(0, S, U - S)]))),
        "c2": striped(np.random.permutation(np.concatenate([np.arange(S), np.random.randint(0, S, U - S)]))),
    }


def reference(x_words, x_scales, w1_words, w1_scales, wm, unit, w2_words, w2_scales, offs, c1, c2):
    xq = unpack_weight(x_words, x_scales)[:, unstriped(offs)]
    y = unpack_fp4(w1_words, w1_scales).T @ xq
    y1 = y[:, unstriped(c1)]
    y2 = y[:, unstriped(c2)]
    hid = f64(unit) * (np.maximum(y1, f64(wm)) + np.minimum(y2, f64(wm)))
    out_0 = unpack_fp4(w2_words, w2_scales).T @ mxq(hid, 0, "e4m3")
    return (out_0,) + planes(out_0)

from contextlib import ExitStack

import concourse.mybir as mybir

F32 = mybir.dt.float32
BF16 = mybir.dt.bfloat16
I32 = mybir.dt.int32
U32 = mybir.dt.uint32
U16 = mybir.dt.uint16
U8 = mybir.dt.uint8
FP8X4 = mybir.dt.float8_e4m3fn_x4
FP4X4 = mybir.dt.float4_e2m1fn_x4
ALU = mybir.AluOpType
COPY = mybir.ActivationFunctionType.Copy

P = 128
PACK = 4
K, T, S, H, N, U = 1024, 1024, 512, 512, 512, 1024
PASSES = K // (P * PACK)
BANK = 512
CHUNKS = (256, 256, 256, 128, 128)
ON_VECTOR = 3
WM_TAG = ("big", "big", "picked", "picked", "big")
Y_ON_SCALAR = (0, 2)
DEAL_ON_GPSIMD = ()
E_ON_VECTOR = ()
IL_ON_SCALAR = ()
G_BUFS = 3
ORDER = 1
NG = 0
HS_BUFS = 2
FLOPS = 2 * K * H * S + 2 * H * N * U


def load_scale_rows(queues, plane, scales):
    for q in range(4):
        queues[q].dma_start(
            out=plane[32 * q : 32 * q + 4, :, :].bitcast(I32),
            in_=scales[:, 4 * q : 4 * q + 4, :].rearrange("o r c -> r o c").bitcast(I32),
        )


def interleaved(ap):
    return ap.rearrange("p (c i t) -> p c t i", i=4, t=PACK)


def planar(ap):
    return ap.rearrange("p t (c i) -> p c t i", i=4)


def tile_picked_ymixpal_clip_po_kernel(
    tc, x_words, x_scales, w1_words, w1_scales, wm, unit, w2_words, w2_scales, offs, c1, c2, out_0, out_1, out_2
):
    nc = tc.nc
    with ExitStack() as ctx:
        keep = ctx.enter_context(tc.tile_pool(name="keep", bufs=1))
        ring = ctx.enter_context(tc.tile_pool(name="ring", bufs=2))
        psum = ctx.enter_context(tc.psum_pool(name="psum", bufs=8))

        offs_t = keep.tile([P, S // 16], U16, name="offs_t")
        c1_t = keep.tile([P, U // 16], U16, name="c1_t")
        c2_t = keep.tile([P, U // 16], U16, name="c2_t")
        xw = [ring.tile([P, T], U32, name=f"xw{o}", tag="big", align_bytes=64) for o in range(PASSES)]
        xs = keep.tile([P, T], U8, name="xs", tag="xs", align_bytes=64)
        w1w = keep.tile([P, PASSES, 2 * H], U8, name="w1w", tag="ww", align_bytes=64)
        w1s = keep.tile([P, PASSES, H], U8, name="w1s", tag="ws", align_bytes=64)
        u4 = keep.tile([P, PACK], F32, name="u4")
        starts = [sum(CHUNKS[:i]) for i in range(len(CHUNKS))]

        xsg = [keep.tile([P, S], U8, name=f"xsg{o}", align_bytes=64) for o in range(PASSES)]
        nc.vector.memset(xs[:].bitcast(I32), 0)
        nc.gpsimd.memset(w1s[:].bitcast(I32), 0)
        nc.vector.memset(xsg[1][:].bitcast(I32), 0)

        wm_v = wm.rearrange("(p t) r -> p t r", t=PACK)
        out_v = out_0.rearrange("(p t) r -> p t r", t=PACK)

        nc.sync.dma_start(offs_t[:], offs)
        nc.sync.dma_start(c1_t[:], c1)
        nc.sync.dma_start(c2_t[:], c2)
        for q in range(4):
            nc.sync.dma_start(
                out=xs[32 * q : 32 * q + 8, :].bitcast(I32), in_=x_scales[:, 4 * q : 4 * q + 4, :].bitcast(I32)
            )
        nc.sync.dma_start(xw[0][:].bitcast(I32), x_words[0].rearrange("p c r -> p (c r)").bitcast(I32))
        if ORDER == 0:
            nc.sync.dma_start(xw[1][:].bitcast(I32), x_words[1].rearrange("p c r -> p (c r)").bitcast(I32))
        if ORDER == 2:
            nc.sync.dma_start(w1w[:].bitcast(I32), w1_words.rearrange("o p c -> p o c").bitcast(I32))
            nc.sync.dma_start(xw[1][:].bitcast(I32), x_words[1].rearrange("p c r -> p (c r)").bitcast(I32))
        load_scale_rows([nc.gpsimd] * NG + [nc.sync] * (4 - NG), w1s, w1_scales)
        if ORDER != 2:
            nc.sync.dma_start(w1w[:].bitcast(I32), w1_words.rearrange("o p c -> p o c").bitcast(I32))
        if ORDER == 1:
            nc.sync.dma_start(xw[1][:].bitcast(I32), x_words[1].rearrange("p c r -> p (c r)").bitcast(I32))
        nc.sync.dma_start(u4[:], unit.rearrange("(p t) o -> p (t o)", t=PACK))

        xg = [ring.tile([P, S], U32, name=f"xg{o}", tag="picked", align_bytes=64) for o in range(PASSES)]
        nc.vector.tensor_copy(xsg[0][:], xs[:].indirect(offs_t[:]))
        for q in range(4):
            nc.scalar.dma_start(
                out=xsg[1][32 * q : 32 * q + 4, :].bitcast(I32), in_=xsg[0][32 * q + 4 : 32 * q + 8, :].bitcast(I32)
            )
        for o in range(PASSES):
            nc.vector.tensor_copy(xg[o][:], xw[o][:].indirect(offs_t[:]))

        def deal(eng, words, scales, passes, t, name):
            dw = keep.tile([P, passes, 2 * P], U8, name=f"{name}w{t}", align_bytes=64)
            ds = keep.tile([P, passes, P], U8, name=f"{name}s{t}", align_bytes=64)
            eng.tensor_copy(
                dw[:].rearrange("p o (m e) -> p o m e", e=2),
                words[:].rearrange("p o (m t e) -> p t o m e", t=PACK, e=2)[:, t],
            )
            eng.tensor_copy(ds[:], scales[:].rearrange("p o (m t) -> p t o m", t=PACK)[:, t])
            return dw, ds

        y = []
        for t in range(PACK):
            dw, ds = deal(nc.gpsimd if t in DEAL_ON_GPSIMD else nc.vector, w1w, w1s, PASSES, t, "w1d")
            acc = psum.tile([P, S], F32, name=f"yacc{t}", tag="bank")
            for o in range(PASSES):
                nc.tensor.matmul_mx(
                    out=acc[:],
                    lhsT=dw[:, o, :].bitcast(FP4X4),
                    lhsT_scale=ds[:, o, :],
                    rhs=xg[o][:].bitcast(FP8X4),
                    rhs_scale=xsg[o][:],
                    start=(o == 0),
                    stop=(o == PASSES - 1),
                )
            yt = keep.tile([P, S], F32, name=f"y{t}", align_bytes=64)
            if t in Y_ON_SCALAR:
                nc.scalar.copy(yt[:], acc[:])
            else:
                nc.vector.tensor_copy(yt[:], acc[:])
            y.append(yt)

        w2w = keep.tile([P, 1, 2 * N], U8, name="w2w", align_bytes=64)
        w2s = keep.tile([P, 1, N], U8, name="w2s", tag="xs", align_bytes=64)
        nc.gpsimd.memset(w2s[:].bitcast(I32), 0)
        nc.sync.dma_start(w2w[:].bitcast(I32), w2_words.rearrange("o p c -> p o c").bitcast(I32))
        load_scale_rows([nc.sync] * 4, w2s, w2_scales)
        w2dw = keep.tile([P, PACK, 2 * P], U8, name="w2dw", align_bytes=64)
        w2ds = keep.tile([P, PACK, P], U8, name="w2ds", align_bytes=64)
        eng2 = nc.gpsimd if 4 in DEAL_ON_GPSIMD else nc.vector
        eng2.tensor_copy(
            w2dw[:].rearrange("p t (m e) -> p t m e", e=2),
            w2w[:, 0, :].rearrange("p (m t e) -> p t m e", t=PACK, e=2),
        )
        eng2.tensor_copy(w2ds[:], w2s[:, 0, :].rearrange("p (m t) -> p t m", t=PACK))

        def fetch(i):
            n = CHUNKS[i]
            cols = slice(starts[i] // 16, (starts[i] + n) // 16)
            g = ring.tile([P, 2, PACK, n], F32, name=f"g{i}", tag="g", bufs=G_BUFS, align_bytes=64)
            for t in range(PACK):
                nc.scalar.activation(g[:, 0, t, :], y[t][:].indirect(c1_t[:, cols]), COPY)
                if i * PACK + t < ON_VECTOR:
                    nc.vector.tensor_copy(g[:, 1, t, :], y[t][:].indirect(c2_t[:, cols]))
                else:
                    nc.scalar.activation(g[:, 1, t, :], y[t][:].indirect(c2_t[:, cols]), COPY)
            return g

        def combine(i, g):
            n = CHUNKS[i]
            w = ring.tile([P, PACK, n], F32, name=f"wm{i}", tag=WM_TAG[i], align_bytes=64)
            nc.sync.dma_start(w[:], wm_v[:, :, starts[i] : starts[i] + n])
            for h in range(2):
                ts = slice(2 * h, 2 * h + 2)
                nc.vector.tensor_tensor(g[:, 0, ts, :], g[:, 0, ts, :], w[:, ts, :], ALU.max)
                nc.vector.tensor_tensor(g[:, 1, ts, :], g[:, 1, ts, :], w[:, ts, :], ALU.min)
            for h in range(2):
                ts = slice(2 * h, 2 * h + 2)
                nc.vector.tensor_tensor(g[:, 0, ts, :], g[:, 0, ts, :], g[:, 1, ts, :], ALU.add)
            hid = ring.tile([P, PACK * n], BF16, name=f"hid{i}", tag="half", align_bytes=64)
            nc.vector.tensor_tensor(
                interleaved(hid[:]),
                planar(g[:, 0, :, :]),
                u4[:].unsqueeze(1).unsqueeze(3).to_broadcast([P, n // 4, PACK, 4]),
                ALU.mult,
            )
            hw = ring.tile([P, n], U32, name="hw", align_bytes=64)
            hs = keep.tile([P, n], U8, name=f"hs{i}", tag="hs", bufs=HS_BUFS, align_bytes=64)
            nc.vector.quantize_mx(out=hw[:].bitcast(FP8X4), scales=hs[:], in_=hid[:])
            per_bank = BANK // n
            banks = []
            for b in range(PACK // per_bank):
                acc = psum.tile([P, per_bank, n], F32, name=f"oacc{i}_{b}", tag="bank")
                for j in range(per_bank):
                    t = b * per_bank + j
                    nc.tensor.matmul_mx(
                        out=acc[:, j, :],
                        lhsT=w2dw[:, t, :].bitcast(FP4X4),
                        lhsT_scale=w2ds[:, t, :],
                        rhs=hw[:].bitcast(FP8X4),
                        rhs_scale=hs[:],
                        start=True,
                        stop=True,
                    )
                banks.append(acc)
            return banks

        def empty(i, banks):
            n = CHUNKS[i]
            per_bank = BANK // n
            o = keep.tile([P, PACK, n], F32, name=f"o{i}", align_bytes=64)
            for b, acc in enumerate(banks):
                if i in E_ON_VECTOR:
                    nc.vector.tensor_copy(o[:, b * per_bank : (b + 1) * per_bank, :], acc[:])
                else:
                    nc.scalar.copy(o[:, b * per_bank : (b + 1) * per_bank, :], acc[:])
            nc.sync.dma_start(out_v[:, :, starts[i] : starts[i] + n], o[:])
            return o

        def hand_on(i, o, out_words, out_scales):
            n = CHUNKS[i]
            cols = slice(starts[i], starts[i] + n)
            ob = ring.tile([P, PACK * n], BF16, name=f"ob{i}", tag="half" if i not in IL_ON_SCALAR else f"ob{i}", align_bytes=64)
            if i in IL_ON_SCALAR:
                nc.scalar.copy(interleaved(ob[:]), planar(o[:]))
            else:
                nc.vector.tensor_copy(interleaved(ob[:]), planar(o[:]))
            nc.vector.quantize_mx(out=out_words[:, cols].bitcast(FP8X4), scales=out_scales[:, cols], in_=ob[:])

        last = len(CHUNKS) - 1
        fetched = [fetch(i) for i in range(G_BUFS)]
        outs = []
        for i in range(last + 1):
            outs.append(empty(i, combine(i, fetched[i])))
            if i + G_BUFS <= last:
                fetched.append(fetch(i + G_BUFS))
        out_scales = keep.tile([P, U], U8, name="out_scales", tag="hs", bufs=HS_BUFS, align_bytes=64)
        out_words = keep.tile([P, U], U32, name="out_words", align_bytes=64)
        words_v = out_1[0].rearrange("p c r -> p (c r)").bitcast(I32)
        for i in range(last + 1):
            hand_on(i, outs[i], out_words, out_scales)
            if i == 1:
                nc.scalar.dma_start(words_v[:, : U // 2], out_words[:, : U // 2].bitcast(I32))
        nc.scalar.dma_start(words_v[:, U // 2 :], out_words[:, U // 2 :].bitcast(I32))
        for q in range(4):
            nc.sync.dma_start(
                out_2[0, 4 * q : 4 * q + 4, :].bitcast(I32), out_scales[32 * q : 32 * q + 4, :].bitcast(I32)
            )
